import numpy as np
import ml_dtypes


def mxq(x, axis, fmt="e4m3"):
    dtype, down = {"e4m3": (ml_dtypes.float8_e4m3fn, 7), "e5m2": (ml_dtypes.float8_e5m2, 14)}[fmt]
    v = np.moveaxis(np.asarray(x, np.float32).astype(ml_dtypes.bfloat16).astype(np.float64), axis, -1)
    blocks = v.reshape(v.shape[:-1] + (-1, 32))
    amax = np.abs(blocks).max(-1, keepdims=True)
    byte = np.maximum(np.where(amax > 0, np.frexp(amax)[1] - 1 + 127, 0) - down, 1)
    scale = np.exp2(byte - 127.0)
    codes = (blocks / scale).astype(np.float32).astype(dtype).astype(np.float64)
    return np.moveaxis((codes * scale).reshape(v.shape), -1, axis)


WIDE = False


def mx_kscale(k):
    if not WIDE:
        return np.ones(k)
    levels = np.array([10, -10, 5, -5, 0])
    if k % 512:
        return np.exp2(np.random.permutation(np.resize(levels, k // 32))).repeat(32)
    a = np.empty((k // 512, 16))
    for p in range(k // 512):
        a[p, :8] = np.random.permutation(np.resize(levels, 8))
        for g in range(8):
            far = levels[np.abs(levels - a[p, g]) >= 10]
            a[p, g + 8] = far[np.random.randint(len(far))]
    return np.exp2(a.ravel()).repeat(32)


BF16 = ml_dtypes.bfloat16


def bf(x):
    return np.asarray(x, np.float32).astype(BF16)


def f64(x):
    return np.asarray(x).astype(np.float64)


E2M1 = np.array([0.0, 0.5, 1.0, 1.5, 2.0, 3.0, 4.0, 6.0, -0.0, -0.5, -1.0, -1.5, -2.0, -3.0, -4.0, -6.0])


def pack_weight(w, fmt):
    k, n = w.shape
    w = f64(bf(w)).reshape(k // 32, 32, n)
    amax = np.abs(w).max(1)
    if fmt == "e4m3":
        byte = np.frexp(amax)[1] - 1 + 127 - 7
    else:
        mant, ex = np.frexp(amax / 6.0)
        byte = np.where(mant > 0.5, ex, ex - 1) + 127
    byte = np.clip(np.where(amax > 0, byte, 1), 1, 254)
    scaled = (w * np.exp2(127.0 - byte)[:, None, :]).reshape(k, n).astype(np.float32)
    by_word = np.ascontiguousarray(scaled.reshape(k // 512, 128, 4, n).transpose(0, 1, 3, 2))
    if fmt == "e4m3":
        words = by_word.astype(ml_dtypes.float8_e4m3fn).view(np.uint8)
    else:
        c = by_word.astype(ml_dtypes.float4_e2m1fn).view(np.uint8) & 0xF
        words = c[..., 0::2] | (c[..., 1::2] << 4)
    return np.ascontiguousarray(words), np.ascontiguousarray(byte.astype(np.uint8).reshape(k // 512, 16, n))


def unpack_weight(words, scales, fmt):
    g, p, n, _ = words.shape
    if fmt == "e4m3":
        vals = np.ascontiguousarray(words).view(ml_dtypes.float8_e4m3fn).astype(np.float64)
    else:
        nib = np.empty((g, p, n, 4), np.uint8)
        nib[..., 0::2] = words & 0xF
        nib[..., 1::2] = words >> 4
        vals = E2M1[nib]
    vals = vals * np.repeat(np.exp2(scales.astype(np.float64) - 127.0), 8, axis=1)[..., None]
    return vals.transpose(0, 1, 3, 2).reshape(g * 512, n)
def pack4(w):
    words, scales = pack_weight(w, "e2m1")
    return words.reshape(words.shape[0], 128, -1), scales


def unpack4(words, scales):
    return unpack_weight(words.reshape(words.shape[0], 128, -1, 2), scales, "e2m1")


def planes(Y):
    n, m = Y.shape
    b = f64(bf(Y)).reshape(n // 32, 32, m)
    amax = np.abs(b).max(1)
    byte = np.clip(np.where(amax > 0, np.frexp(amax)[1] - 1 + 127 - 7, 1), 1, 254)
    codes = (b * np.exp2(127.0 - byte)[:, None, :]).reshape(n, m).astype(np.float32).astype(ml_dtypes.float8_e4m3fn).view(np.uint8)
    words = codes.reshape(n // 512, 128, 4, m).transpose(0, 1, 3, 2)
    return np.ascontiguousarray(words), np.ascontiguousarray(byte.astype(np.uint8).reshape(n // 512, 16, m))


NIMG, KLOW, KHIGH, NCLS, NF = 2048, 512, 1024, 512, 1536

def setup_inputs():
    rn = np.random.standard_normal
    s_low, s_high, t = mx_kscale(KLOW), mx_kscale(KHIGH), mx_kscale(NIMG)
    freq = (np.arange(NF) + 0.5) / NF
    ctf = -np.sin(4.0 * np.pi * freq ** 2 + 0.1)
    ref = ctf[:, None] * rn((NF, NCLS))
    ref = ref / np.sqrt((ref ** 2).sum(axis=0, keepdims=True))
    words, scales = pack4(ref[KLOW:] / s_high[:, None])
    white = rn((NIMG, NF))
    spectrum = np.exp(0.4 * rn(NF))
    gain = 0.5 * np.exp(0.7 * rn(NF))
    return {
        "x_low": bf(white[:, :KLOW] * s_low),
        "x_high": bf(white[:, KLOW:] * s_high),
        "ref_low": bf(ref[:KLOW] / s_low[:, None]),
        "ref_high_words": words, "ref_high_scales": scales,
        "image_weight": bf(NCLS / np.sqrt(NIMG) * np.exp(0.3 * rn(NIMG)) * t),
        "spectra": bf(white * spectrum / t[:, None]),
        "gain": bf(gain),
        "kept": bf(rn((NCLS, NF)) * gain),
    }

def reference(x_low, x_high, ref_low, ref_high_words, ref_high_scales, image_weight, spectra, gain, kept):
    low = mxq(f64(x_low), 1, "e4m3") @ mxq(f64(ref_low), 0, "e4m3")
    high = mxq(f64(x_high), 1, "e4m3") @ unpack4(ref_high_words, ref_high_scales)
    score = low + high
    e = np.exp(score - score.max(axis=1, keepdims=True))
    h = e / e.sum(axis=1, keepdims=True) * f64(image_weight)[:, None]
    sums = mxq(h, 0, "e4m3").T @ mxq(f64(spectra), 0, "e4m3")
    y = sums * f64(gain) + f64(kept)
    words, scales = planes(y.T)
    return y, words, scales

from contextlib import ExitStack

import concourse.mybir as mybir
from concourse.masks import make_identity

NIMG, KLOW, KHIGH, NCLS, NF = 2048, 512, 1024, 512, 1536
FLOPS = 2 * NIMG * (KLOW + KHIGH) * NCLS + 2 * NIMG * NCLS * NF

F32 = mybir.dt.float32
BF16 = mybir.dt.bfloat16
I32 = mybir.dt.int32
U32 = mybir.dt.uint32
U8 = mybir.dt.uint8
FP8X4 = mybir.dt.float8_e4m3fn_x4
FP4X4 = mybir.dt.float4_e2m1fn_x4
ALU = mybir.AluOpType
ACT = mybir.ActivationFunctionType

P = 128
PACK = 4
KP = P * PACK
IMG_GROUPS = NIMG // KP
F_GROUPS = NF // KP
PAIRS = 2 * IMG_GROUPS
CBLOCKS = NCLS // P
ORDER = [
    ("ll", 0),
    ("xt", 0, 0),
    ("xc", 0, 0, "S"),
    ("lh", 0),
    ("lm", "rl0"),
    ("xt", 0, 1),
    ("lm", "rs"),
    ("ll", 1),
    ("rc", 0, "V"),
    ("xt", 0, 2),
    ("xt", 1, 0),
    ("lh", 1),
    ("lm", "rl1"),
    ("xc", 0, 1, "S"),
    ("xc", 0, 2, "V"),
    ("xt", 1, 1),
    ("xq", 0, 0, 1),
    ("xq", 0, 1, 3),
    ("rc", 1, "V"),
    ("lm", "rw"),
    ("xc", 1, 0, "S"),
    ("xc", 1, 1, "S"),
    ("xq", 1, 0, 1),
    ("xt", 1, 2),
    ("ls", 0, 0),
    ("xc", 1, 2, "S"),
    ("rq",),
    ("cs", 0, 0, 0, "V"),
    ("sc", 0, 0),
    ("sc", 0, 1),
    ("ls", 1, 0),
    ("ll", 2),
    ("xq", 1, 1, 3),
    ("cs", 0, 0, 1, "S"),
    ("cs", 1, 0, 0, "S"),
    ("sc", 1, 0),
    ("lh", 2),
    ("mx", 0, 0),
    ("cs", 1, 0, 1, "V"),
    ("ll", 3),
    ("lh", 3),
    ("xt", 2, 0),
    ("mx", 0, 1),
    ("xt", 2, 1),
    ("ex", 0, 0),
    ("xt", 2, 2),
    ("xc", 2, 0, "S"),
    ("sc", 1, 1),
    ("ls", 2, 0),
    ("xc", 2, 1, "S"),
    ("xc", 2, 2, "S"),
    ("qs", 0, 0, 1),
    ("xt", 3, 0),
    ("xt", 3, 1),
    ("xq", 2, 0, 1),
    ("mx", 1, 0),
    ("mx", 1, 1),
    ("xq", 2, 1, 3),
    ("ex", 0, 1),
    ("cs", 2, 0, 2, "V"),
    ("xt", 3, 2),
    ("ex", 1, 0),
    ("xc", 3, 0, "S"),
    ("sc", 2, 0),
    ("sc", 2, 1),
    ("ls", 3, 0),
    ("xq", 3, 0, 1),
    ("ex", 1, 1),
    ("xc", 3, 1, "S"),
    ("ll", 4),
    ("lh", 4),
    ("xc", 3, 2, "S"),
    ("re", 0),
    ("xt", 4, 0),
    ("lm", "w"),
    ("xt", 4, 1),
    ("cs", 3, 0, 0, "V"),
    ("lh", 5),
    ("xt", 4, 2),
    ("cs", 3, 0, 1, "S"),
    ("mx", 2, 0),
    ("ll", 5),
    ("xq", 3, 1, 3),
    ("ex", 2, 0),
    ("xc", 4, 0, "S"),
    ("fa", 0),
    ("xc", 4, 1, "S"),
    ("mx", 2, 1),
    ("qs", 2, 0, 1),
    ("xq", 4, 0, 1),
    ("xc", 4, 2, "S"),
    ("ls", 0, 1),
    ("lh", 6),
    ("ll", 6),
    ("ll", 7),
    ("lh", 7),
    ("sc", 3, 0),
    ("sc", 3, 1),
    ("mx", 3, 0),
    ("ex", 2, 1),
    ("ex", 3, 0),
    ("xq", 4, 1, 3),
    ("xt", 5, 0),
    ("xt", 5, 1),
    ("mx", 3, 1),
    ("xt", 5, 2),
    ("lm", "kept"),
    ("xc", 5, 0, "S"),
    ("hs", 0, 2),
    ("sc", 4, 0),
    ("xc", 5, 1, "S"),
    ("ex", 3, 1),
    ("xq", 5, 0, 1),
    ("re", 1),
    ("mx", 4, 0),
    ("sc", 4, 1),
    ("xt", 6, 0),
    ("xc", 5, 2, "S"),
    ("xt", 6, 1),
    ("xt", 6, 2),
    ("xq", 5, 1, 3),
    ("cs", 0, 1, 0, "S"),
    ("fa", 1),
    ("xc", 6, 0, "S"),
    ("xt", 7, 0),
    ("mx", 4, 1),
    ("sc", 5, 0),
    ("lm", "gain"),
    ("ls", 1, 1),
    ("xc", 6, 1, "S"),
    ("ex", 4, 0),
    ("xc", 6, 2, "S"),
    ("ex", 4, 1),
    ("hs", 1, 2),
    ("mx", 5, 0),
    ("xc", 7, 0, "S"),
    ("xq", 6, 0, 1, 1),
    ("xt", 7, 1),
    ("xc", 7, 1, "S"),
    ("xt", 7, 2),
    ("xc", 7, 2, "S"),
    ("xq", 6, 1, 3, 1),
    ("ex", 5, 0),
    ("kt", 0, 0),
    ("kc", 0, 0, "S"),
    ("cs", 0, 1, 1, "S"),
    ("sc", 5, 1),
    ("sc", 6, 0),
    ("sc", 6, 1),
    ("mx", 5, 1),
    ("cs", 1, 1, 0, "V"),
    ("mx", 6, 0),
    ("hq", 0),
    ("ex", 5, 1),
    ("sc", 7, 0),
    ("mx", 6, 1),
    ("re", 2),
    ("cs", 1, 1, 1, "S"),
    ("mx", 7, 0),
    ("ex", 6, 0),
    ("sc", 7, 1),
    ("ex", 6, 1),
    ("fa", 2),
    ("ex", 7, 0),
    ("mx", 7, 1),
    ("hs", 2, 2),
    ("ls", 2, 1),
    ("ls", 3, 1),
    ("kt", 0, 1),
    ("ex", 7, 1),
    ("re", 3),
    ("hq", 1),
    ("kc", 0, 1, "S"),
    ("kt", 1, 0),
    ("fa", 3),
    ("kc", 1, 0, "S"),
    ("hq", 2),
    ("kt", 1, 1),
    ("hs", 3, 2),
    ("ls", 0, 2),
    ("kc", 1, 1, "S"),
    ("cs", 2, 1, 2, "S"),
    ("cs", 3, 1, 2, "S"),
    ("su", 0, 0, 0, 3),
    ("su", 0, 1, 0, 3),
    ("cs", 0, 2, 0, "V"),
    ("hq", 3),
    ("su", 0, 2, 0, 3),
    ("qs", 0, 1, 1),
    ("su", 0, 3, 0, 3),
    ("cs", 0, 2, 1, "S"),
    ("ls", 1, 2),
    ("kt", 2, 0),
    ("su", 0, 0, 3, 4),
    ("cs", 1, 2, 2, "S"),
    ("qs", 2, 1, 1),
    ("su", 0, 1, 3, 4),
    ("ym", 0, 0),
    ("su", 0, 2, 3, 4),
    ("ym", 0, 1),
    ("su", 0, 3, 3, 4),
    ("su", 1, 0, 0, 4),
    ("ym", 0, 2),
    ("su", 1, 1, 0, 4),
    ("ym", 0, 3),
    ("kc", 2, 0, "S"),
    ("kt", 2, 1),
    ("yt", 0, 0),
    ("ls", 2, 2),
    ("cs", 2, 2, 2, "V"),
    ("ym", 1, 0),
    ("ls", 3, 2),
    ("cs", 3, 2, 2, "S"),
    ("qs", 0, 2, 1),
    ("kc", 2, 1, "S"),
    ("yo", 0, 0, "S"),
    ("yt", 0, 1),
    ("su", 1, 2, 0, 4),
    ("yo", 0, 1, "S"),
    ("ym", 1, 1),
    ("yc", 0, 0, "S"),
    ("yt", 0, 2),
    ("yt", 0, 3),
    ("su", 1, 3, 0, 4),
    ("st", 0, 0, 2),
    ("qs", 2, 2, 1),
    ("su", 2, 0, 0, 4, 0, 256),
    ("su", 2, 1, 0, 4, 0, 256),
    ("ym", 1, 2),
    ("yo", 0, 2, "S"),
    ("yc", 0, 1, "V"),
    ("ym", 1, 3),
    ("yo", 0, 3, "V"),
    ("su", 2, 2, 0, 4, 0, 256),
    ("yt", 1, 0),
    ("yt", 1, 1),
    ("yt", 1, 2),
    ("st", 0, 2, 4),
    ("yo", 1, 0, "S"),
    ("yo", 1, 1, "S"),
    ("yq", 0),
    ("yt", 1, 3),
    ("su", 2, 3, 0, 4, 0, 256),
    ("ym", 2, 0, 0, 256),
    ("su", 2, 0, 0, 4, 256, 512),
    ("ym", 2, 1, 0, 256),
    ("ym", 2, 2, 0, 256),
    ("su", 2, 1, 0, 4, 256, 512),
    ("yc", 1, 0, "V"),
    ("ym", 2, 3, 0, 256),
    ("su", 2, 2, 0, 4, 256, 512),
    ("yc", 1, 1, "S"),
    ("yo", 1, 2, "S"),
    ("yt", 2, 0),
    ("yo", 1, 3, "V"),
    ("yc", 2, 0, "S"),
    ("yo", 2, 0, "S"),
    ("s1", 0),
    ("yt", 2, 1),
    ("st", 1, 0, 2),
    ("yo", 2, 1, "S"),
    ("ym", 2, 0, 256, 512),
    ("st", 1, 2, 4),
    ("su", 2, 3, 0, 4, 256, 512),
    ("yq", 1),
    ("ym", 2, 1, 256, 512),
    ("ym", 2, 2, 256, 512),
    ("yq", 2, 0, 256),
    ("ym", 2, 3, 256, 512),
    ("s1", 1),
    ("yc", 2, 1, "V"),
    ("yt", 2, 2),
    ("s1", 2, 0, 256),
    ("yq", 2, 256, 512),
    ("yt", 2, 3),
    ("st", 2, 0, 2),
    ("yo", 2, 2, "S"),
    ("yo", 2, 3, "S"),
    ("st", 2, 2, 3),
    ("s1", 2, 256, 512),
    ("s2",),
    ("st", 2, 3, 4),
]


def tile_ctf_softmax_class_sums_k6_kernel(
    tc, x_low, x_high, ref_low, ref_high_words, ref_high_scales, image_weight, spectra, gain, kept, out_0, out_1, out_2
):
    nc = tc.nc
    with ExitStack() as ctx:
        keep = ctx.enter_context(tc.tile_pool(name="keep", bufs=1))
        work = ctx.enter_context(tc.tile_pool(name="work", bufs=2))
        psum = ctx.enter_context(tc.psum_pool(name="psum", bufs=4))
        ctx.enter_context(tc.manual_schedule())

        ident = keep.tile([P, P], F32, name="ident")
        make_identity(nc, ident[:])
        rh_scales = keep.tile([P, 2, NCLS], U8, name="rh_scales", align_bytes=64)
        nc.vector.memset(rh_scales[:].rearrange("p g n -> p (g n)").bitcast(I32), 0)
        zeros = keep.tile([P, NCLS], BF16, name="zeros")
        nc.vector.memset(zeros[:], 0.0)
        warm = keep.tile([P, 8], F32, name="warm")
        nc.vector.memset(warm[:, 0:1], 0.0)
        nc.scalar.activation(out=warm[:, 1:2], in_=warm[:, 0:1], func=ACT.Exp)

        xl, xh, sraw, xg, xc, xs, score = {}, {}, {}, {}, {}, {}, {}
        tbank, sg, acc, obank, kbank = {}, {}, {}, {}, {}
        nmax, rsum, e, hb, rr = {}, {}, {}, {}, {}
        yt, yb, yc, ys = {}, {}, {}, {}

        def load_low(h):
            g, t0 = h // 2, 2 * (h % 2)
            xl[h] = work.tile([P, 2, KLOW], BF16, name=f"xl{h}", tag="xl", bufs=3)
            nc.sync.dma_start(out=xl[h][:], in_=x_low[KP * g : KP * (g + 1), :].rearrange("(p t) k -> p t k", t=PACK)[:, t0 : t0 + 2, :])

        def load_high(h):
            g, t0 = h // 2, 2 * (h % 2)
            xh[h] = work.tile([P, 2, KHIGH], BF16, name=f"xh{h}", tag="xh", bufs=3)
            nc.sync.dma_start(out=xh[h][:], in_=x_high[KP * g : KP * (g + 1), :].rearrange("(p t) k -> p t k", t=PACK)[:, t0 : t0 + 2, :])

        def load_spectra(g, fg):
            sraw[g, fg] = work.tile([P, PACK, KP], BF16, name=f"sraw{g}_{fg}", tag="sraw", bufs=7)
            src = spectra[KP * g : KP * (g + 1), KP * fg : KP * (fg + 1)]
            nc.sync.dma_start(out=sraw[g, fg][:], in_=src.rearrange("(p j) f -> p j f", j=PACK))

        rl_raw = {w: keep.tile([P, PACK, NCLS // 2], BF16, name=w) for w in ("rl0", "rl1")}
        rh_words = keep.tile([P, 2, 2 * NCLS], U8, name="rh_words", align_bytes=64)
        weight = keep.tile([P, IMG_GROUPS, PACK], BF16, name="weight")
        gain_sb = keep.tile([P, F_GROUPS, PACK], BF16, name="gain_sb")
        kept_raw = keep.tile([P, CBLOCKS, NF], BF16, name="kept_raw")

        rl_codes = keep.tile([P, NCLS], U32, name="rl_codes", align_bytes=64)
        rl_scales = keep.tile([P, NCLS], U8, name="rl_scales", align_bytes=64)
        rl_g = keep.tile([P, NCLS * PACK], BF16, name="rl_g", align_bytes=64)
        h_codes = keep.tile([P, IMG_GROUPS, NCLS], U32, name="h_codes", align_bytes=64)
        h_scales = keep.tile([P, IMG_GROUPS, NCLS], U8, name="h_scales", align_bytes=64)
        s_codes = keep.tile([P, F_GROUPS, IMG_GROUPS, KP], U32, name="s_codes", align_bytes=64)
        s_scales = keep.tile([P, F_GROUPS, IMG_GROUPS, KP], U8, name="s_scales", align_bytes=64)
        kept_t = keep.tile([P, F_GROUPS, 2, NCLS, 2], BF16, name="kept_t")

        def x_transposes(h, b):
            tbank[h, b] = psum.tile([P, 2, 2, P], F32, name=f"tb{h}_{b}", tag="T")
            for s in range(2):
                row = xl[h][:, s, :] if b == 0 else xh[h][:, b - 1, KP * s : KP * (s + 1)]
                words = row.bitcast(F32)
                for u in range(2):
                    nc.tensor.transpose(tbank[h, b][:, s, u, :], words[:, u : 2 * P : 2], ident[:])

        def copy_on(eng, out, in_):
            if eng == "V":
                nc.vector.tensor_copy(out=out, in_=in_)
            elif eng == "G":
                nc.gpsimd.tensor_scalar(out=out, in0=in_, scalar1=1.0, scalar2=0.0, op0=ALU.mult, op1=ALU.add)
            else:
                nc.scalar.copy(out=out, in_=in_)

        def x_slot(h, b):
            return h % 2 if b == 0 else 2 * (h % 2) + b + 1

        def x_copy(h, b, eng):
            g, n = h // 2, x_slot(h, b)
            if g not in xg:
                xg[g] = work.tile([P, 12 * KP], BF16, name=f"xg{g}", tag="xg", align_bytes=64)
            dst = xg[g][:, 2 * KP * n : 2 * KP * (n + 1)].bitcast(F32)
            copy_on(eng, dst.rearrange("p (s r u) -> p s r u", s=2, u=2), tbank[h, b][:].rearrange("p s u r -> p s r u"))

        def x_quant(h, b0, b1, both=0):
            g = h // 2
            if g not in xc:
                xc[g] = work.tile([P, 12 * P], U32, name=f"xc{g}", tag="xc", align_bytes=64)
                xs[g] = work.tile([P, 12 * P], U8, name=f"xs{g}", tag="xs", align_bytes=64)
            n0 = x_slot(h, b0)
            n1 = n0 + (b1 - b0) * (1 + both)
            cols = slice(2 * P * n0, 2 * P * n1)
            nc.vector.quantize_mx(out=xc[g][:, cols].bitcast(FP8X4), scales=xs[g][:, cols], in_=xg[g][:, 2 * KP * n0 : 2 * KP * n1])

        def scores(h, a):
            g = h // 2
            score[h, a] = psum.tile([P, NCLS], F32, name=f"score{h}_{a}", tag="S")
            for s in range(2):
                n = 2 * x_slot(h, 1 + a) + s
                cols = slice(P * n, P * (n + 1))
                nc.tensor.matmul_mx(out=score[h, a][:], lhsT=xc[g][:, cols].bitcast(FP8X4), lhsT_scale=xs[g][:, cols],
                                    rhs=rh_words[:, s, :].bitcast(FP4X4), rhs_scale=rh_scales[:, s, :], start=(s == 0), stop=False)
            n = 2 * x_slot(h, 0) + a
            cols = slice(P * n, P * (n + 1))
            nc.tensor.matmul_mx(out=score[h, a][:], lhsT=xc[g][:, cols].bitcast(FP8X4), lhsT_scale=xs[g][:, cols],
                                rhs=rl_codes[:].bitcast(FP8X4), rhs_scale=rl_scales[:], start=False, stop=True)

        def keep_warm(n, name):
            if n:
                bank = psum.tile([P, NCLS], F32, name=name, tag="T")
                for k in range(n):
                    nc.tensor.matmul(out=bank[:], lhsT=zeros[:, 0:P], rhs=zeros[:], start=True, stop=True)

        def row_max(h, a):
            g, t = h // 2, 2 * (h % 2) + a
            if g not in nmax:
                nmax[g] = work.tile([P, PACK], F32, name=f"nmax{g}", tag="nmax")
            nc.vector.tensor_reduce(out=nmax[g][:, t : t + 1], in_=score[h, a][:], axis=mybir.AxisListType.X, op=ALU.max, negate=True)

        def exps(h, a):
            g, t = h // 2, 2 * (h % 2) + a
            if g not in e:
                e[g] = work.tile([P, PACK, NCLS], F32, name=f"e{g}", tag="wide")
                rsum[g] = work.tile([P, PACK], F32, name=f"rsum{g}", tag="rsum")
            nc.scalar.activation(out=e[g][:, t, :], in_=score[h, a][:], func=ACT.Exp, bias=nmax[g][:, t : t + 1], accum_out=rsum[g][:, t : t + 1])

        def recip(g):
            rr[g] = work.tile([P, 2, PACK], F32, name=f"rr{g}", tag="rr")
            nc.vector.reciprocal(out=rr[g][:, 0, :], in_=rsum[g][:])

        def factor(g):
            nc.vector.tensor_tensor(out=rr[g][:, 1, :], in0=rr[g][:, 0, :], in1=weight[:, g, :], op=ALU.mult)

        def h_scale(g, half):
            if g not in hb:
                hb[g] = work.tile([P, NCLS * PACK], BF16, name=f"hb{g}", tag="cast", align_bytes=64)
            c0, c1 = (0, NCLS) if half == 2 else (256 * half, 256 * (half + 1))
            nc.vector.tensor_tensor(
                out=hb[g][:, PACK * c0 : PACK * c1].rearrange("p (c i t) -> p c t i", i=2, t=PACK),
                in0=e[g][:, :, c0:c1].rearrange("p t (c i) -> p c t i", i=2),
                in1=rr[g][:, 1, :].unsqueeze(1).unsqueeze(3).to_broadcast([P, (c1 - c0) // 2, PACK, 2]),
                op=ALU.mult,
            )

        def h_quant(g):
            nc.vector.quantize_mx(out=h_codes[:, g, :].bitcast(FP8X4), scales=h_scales[:, g, :], in_=hb[g][:])

        def s_copy(g, fg, half, eng):
            if (g // 2, fg) not in sg:
                sg[g // 2, fg] = work.tile([P, 2, KP * PACK], BF16, name=f"sg{g // 2}_{fg}", tag="sg", bufs=3, align_bytes=64)
            ms = slice(0, P) if half == 2 else slice(64 * half, 64 * (half + 1))
            dst = sg[g // 2, fg][:, g % 2, :].rearrange("p (t m j) -> p m j t", t=PACK, j=PACK)[:, ms, :, :]
            src = sraw[g, fg][:].rearrange("p j (m t) -> p m j t", t=PACK)[:, ms, :, :]
            copy_on(eng, dst, src)

        def s_quant(g, fg, both=0):
            gs = slice(g, g + 1 + both)
            nc.vector.quantize_mx(
                out=s_codes[:, fg, gs, :].rearrange("p g n -> p (g n)").bitcast(FP8X4),
                scales=s_scales[:, fg, gs, :].rearrange("p g n -> p (g n)"),
                in_=sg[g // 2, fg][:, g % 2 : g % 2 + 1 + both, :].rearrange("p g n -> p (g n)"),
            )

        def kept_transposes(fg, u):
            kbank[fg, u] = psum.tile([P, CBLOCKS, P], F32, name=f"kb{fg}_{u}", tag="S")
            for b in range(CBLOCKS):
                words = kept_raw[:, b, KP * fg : KP * (fg + 1)].bitcast(F32)
                nc.tensor.transpose(kbank[fg, u][:, b, :], words[:, u : 2 * P : 2], ident[:])

        def kept_copy(fg, u, eng):
            dst = kept_t[:, fg, u, :, :].rearrange("p c e -> p (c e)").bitcast(F32)
            copy_on(eng, dst, kbank[fg, u][:].rearrange("p b c -> p (b c)"))

        def sums(fg, t, g0, g1, c0=0, c1=NCLS):
            if g0 == 0:
                acc[fg, t, c0] = psum.tile([P, c1 - c0], F32, name=f"acc{fg}_{t}_{c0}", tag="T" if fg == 0 else "S")
            cols = slice(P * t, P * (t + 1))
            for g in range(g0, g1):
                nc.tensor.matmul_mx(out=acc[fg, t, c0][:], lhsT=s_codes[:, fg, g, cols].bitcast(FP8X4), lhsT_scale=s_scales[:, fg, g, cols],
                                    rhs=h_codes[:, g, c0:c1].bitcast(FP8X4), rhs_scale=h_scales[:, g, c0:c1], start=(g == 0), stop=(g == IMG_GROUPS - 1))

        def y_make(fg, t, c0=0, c1=NCLS):
            if fg not in yt:
                yt[fg] = work.tile([P, PACK, NCLS], F32, name=f"yt{fg}", tag="wide")
            nc.vector.scalar_tensor_tensor(out=yt[fg][:, t, c0:c1], in0=acc[fg, t, c0][:], scalar=gain_sb[:, fg, t : t + 1],
                                           in1=kept_t[:, fg, t // 2, c0:c1, t % 2], op0=ALU.mult, op1=ALU.add)

        def y_cast(fg, half, eng):
            if fg not in yb:
                yb[fg] = work.tile([P, NCLS * PACK], BF16, name=f"yb{fg}", tag="cast", align_bytes=64)
            c0, c1 = (0, NCLS) if half == 2 else (256 * half, 256 * (half + 1))
            dst = yb[fg][:, PACK * c0 : PACK * c1].rearrange("p (c i t) -> p c t i", i=2, t=PACK)
            src = yt[fg][:, :, c0:c1].rearrange("p t (c i) -> p c t i", i=2)
            copy_on(eng, dst, src)

        y_scales = keep.tile([P, F_GROUPS, NCLS], U8, name="y_scales", align_bytes=64)

        def y_quant(fg, c0=0, c1=NCLS):
            if fg not in yc:
                yc[fg] = work.tile([P, NCLS], U32, name=f"yc{fg}", tag="yc", align_bytes=64)
            nc.vector.quantize_mx(out=yc[fg][:, c0:c1].bitcast(FP8X4), scales=y_scales[:, fg, c0:c1], in_=yb[fg][:, PACK * c0 : PACK * c1])

        def store_codes(fg, c0=0, c1=NCLS):
            nc.sync.dma_start(out=out_1[fg, :, c0:c1, :].rearrange("p m t -> p (m t)").bitcast(I32), in_=yc[fg][:, c0:c1].bitcast(I32))

        def store_scales():
            for q in range(4):
                nc.sync.dma_start(
                    out=out_2[:, 4 * q : 4 * q + 4, :].rearrange("g r m -> r g m").bitcast(I32),
                    in_=y_scales[32 * q : 32 * q + 4, :, :].bitcast(I32),
                )

        def y_transposes(fg, b):
            obank[fg, b] = psum.tile([P, PACK, P], F32, name=f"ob{fg}_{b}", tag="T")
            for t in range(PACK):
                nc.tensor.transpose(obank[fg, b][:, t, :], yt[fg][:, t, P * b : P * (b + 1)], ident[:])

        yo = {}

        def y_copy(fg, b, eng):
            if (fg, b // 2) not in yo:
                yo[fg, b // 2] = work.tile([P, 2, P, PACK], F32, name=f"yo{fg}_{b // 2}", tag="yo", bufs=3)
            copy_on(eng, yo[fg, b // 2][:, b % 2, :, :], obank[fg, b][:].rearrange("c t p -> c p t"))

        def y_store(fg, b0, b1):
            dst = out_0[P * b0 : P * b1, KP * fg : KP * (fg + 1)].rearrange("(b c) f -> c b f", c=P)
            nc.sync.dma_start(out=dst, in_=yo[fg, b0 // 2][:, b0 % 2 : b0 % 2 + b1 - b0].rearrange("c b p t -> c b (p t)"))

        def load_misc(what):
            if what in ("rl0", "rl1"):
                cs = slice(0, 256) if what == "rl0" else slice(256, 512)
                nc.sync.dma_start(out=rl_raw[what][:], in_=ref_low[:, cs].rearrange("(p j) c -> p j c", j=PACK))
            if what == "rw":
                nc.sync.dma_start(out=rh_words[:].bitcast(I32), in_=ref_high_words.rearrange("g p n -> p g n").bitcast(I32))
            if what == "rs":
                for q in range(4):
                    nc.sync.dma_start(
                        out=rh_scales[32 * q : 32 * q + 4, :, :].bitcast(I32),
                        in_=ref_high_scales[:, 4 * q : 4 * q + 4, :].rearrange("g r n -> r g n").bitcast(I32),
                    )
            if what == "w":
                nc.sync.dma_start(out=weight[:], in_=image_weight.rearrange("(g p t) -> p g t", p=P, t=PACK))
            if what == "gain":
                nc.sync.dma_start(out=gain_sb[:], in_=gain.rearrange("(g p t) -> p g t", p=P, t=PACK))
            if what == "kept":
                nc.sync.dma_start(out=kept_raw[:], in_=kept.rearrange("(b p) f -> p b f", p=P))

        def rl_copy(half, eng):
            rl_dst = rl_g[:].rearrange("p (c i t) -> p c t i", i=4, t=PACK)
            rl_src = rl_raw[f"rl{half}"][:].rearrange("p t (c i) -> p c t i", i=4)
            cs = slice(64 * half, 64 * (half + 1))
            copy_on(eng, rl_dst[:, cs], rl_src)

        def rl_quant():
            nc.vector.quantize_mx(out=rl_codes[:].bitcast(FP8X4), scales=rl_scales[:], in_=rl_g[:])

        steps = {
            "ll": load_low, "lh": load_high, "ls": load_spectra, "lm": load_misc, "rc": rl_copy, "rq": rl_quant, "w": keep_warm,
            "xt": x_transposes, "xc": x_copy, "xq": x_quant, "sc": scores, "mx": row_max, "ex": exps,
            "re": recip, "fa": factor, "hs": h_scale, "hq": h_quant, "cs": s_copy, "qs": s_quant,
            "kt": kept_transposes, "kc": kept_copy, "su": sums, "ym": y_make, "yc": y_cast, "yq": y_quant,
            "yt": y_transposes, "yo": y_copy, "st": y_store, "s1": store_codes, "s2": store_scales,
        }
        keep_warm(5, "warm0")
        for item in ORDER:
            steps[item[0]](*item[1:])
